import numpy as np, ml_dtypes
CORES = [2,3,6,7,58,59,62,63,114,115,118,119]
N = 12
F = 128
def setup_inputs(rng):
    return {"x": rng.standard_normal((N, 128, N * F), dtype=np.float32).astype(ml_dtypes.bfloat16), "w": rng.standard_normal((N, 128, 128), dtype=np.float32).astype(ml_dtypes.bfloat16)}
def setup_inputs_big(rng):
    d = setup_inputs(rng)
    for k in ("x", "w"): d[k] = (d[k].astype(np.float32) * 1024.0).astype(d[k].dtype)
    return d
def setup_inputs_small(rng):
    d = setup_inputs(rng)
    for k in ("x", "w"): d[k] = (d[k].astype(np.float32) * (1 / 1024.0)).astype(d[k].dtype)
    return d
def setup_inputs_apart(rng):
    d = setup_inputs(rng)
    f = (10.0 ** rng.permutation(np.linspace(-1.5, 1.5, N))).astype(np.float32).reshape(N, 1, 1)
    for k in ("x", "w"): d[k] = (d[k].astype(np.float32) * f).astype(d[k].dtype)
    return d
def reference(x, w):
    X, W = x.astype(np.float64), w.astype(np.float64)
    s = X.sum(axis=0)
    o = np.concatenate([W[r].T @ s[:, F * r:F * r + F] for r in range(N)], axis=1).astype(ml_dtypes.bfloat16 if x.dtype != np.float64 else np.float64)
    return {"y": np.broadcast_to(o, (N,) + o.shape)}

@@ -1,0 +1,175 @@
+import comms_topo
+from concourse.bass import DstId, RemoteDMATransfer
+
+N, F = 12, 128
+CORES = [2, 3, 6, 7, 58, 59, 62, 63, 114, 115, 118, 119]
+CHIPS = sorted({comms_topo.chip(c) for c in CORES})
+NC = len(CHIPS)
+G = N // NC
+B = N // G
+W = B * F
+
+SCRATCH = {
+    "xs": ("sbuf", [128, N * F], "bfloat16"),
+    "rl": ("sbuf", [128, G * W], "bfloat16"),
+    "xr": ("sbuf", [128, NC * W], "bfloat16"),
+    "wd": ("dram", [128, F], "bfloat16"),
+    "wland": ("dram", [B, 128, F], "bfloat16"),
+    "wsb": ("sbuf", [128, W], "bfloat16"),
+    "yb": ("sbuf", [128, N * F], "bfloat16"),
+}
+for _k in range(B):
+    SCRATCH["ps%d" % _k] = ("psum", [128, 512], "float32")
+
+SEMAPHORES = (["xl", "wl", "ra", "cp", "st", "ls"]
+              + ["wa%d" % k for k in range(B)] + ["ws%d" % k for k in range(B)] + ["mm%d" % k for k in range(B)]
+              + ["xc%d" % a for a in range(NC)] + ["ag%d" % p for p in range(G)])
+
+
+def _bits(mask):
+    return [1 << b for b in range(mask.bit_length()) if (mask >> b) & 1]
+
+
+def _part(mask, i, n):
+    bits = _bits(mask)
+    m = len(bits) // n
+    return sum(bits[i * m:(i + 1) * m])
+
+
+def _common(topo, src, dsts):
+    m = topo.mask(src, dsts[0])
+    for d in dsts[1:]:
+        m &= topo.mask(src, d)
+    return m
+
+
+def _members(topo, cores):
+    return [sorted([c for c in cores if topo.chip(c) == ch], key=lambda c: (topo.die(c), c)) for ch in CHIPS]
+
+
+def _w_plan(topo, mem, cores, src):
+    jr = cores.index(src) // B
+    dests = [mem[a][jr] for a in range(NC) if mem[a][jr] != src]
+    off = [d for d in dests if topo.chip(d) != topo.chip(src)]
+    on = [d for d in dests if topo.chip(d) == topo.chip(src)]
+    plan = [(_common(topo, src, off), off)]
+    if on:
+        plan.append((_common(topo, src, on) & ~plan[0][0], on))
+    return plan
+
+
+def _rs_plan(topo, mem, src):
+    peers = [c for c in mem[CHIPS.index(topo.chip(src))] if c != src]
+    calls = []
+    for grp in ([c for c in peers if topo.die(c) != topo.die(src)], [c for c in peers if topo.die(c) == topo.die(src)]):
+        if grp:
+            n = 1
+            while n < len(grp):
+                n *= 2
+            calls.append([(_part(topo.mask(src, c), i, n), c) for i, c in enumerate(grp)])
+    return calls
+
+
+def rank_program(g, core, T, topo):
+    if T.rank_of(core) is None:
+        return
+    cores = list(T.cores)
+    mem = _members(topo, cores)
+    a = CHIPS.index(topo.chip(core))
+    j = mem[a].index(core)
+    S = T.sem
+    sent = [0]
+
+    def dst(c):
+        assert topo.may_write(core, c)
+        rid, pid, _ = topo.addr(c)
+        return DstId(rid=rid, pnc=pid)
+
+    def sl(t, i):
+        return t[:, i * W:(i + 1) * W]
+
+    def blk(t, i):
+        return t[:, i * F:(i + 1) * F]
+
+    def tr(mask, ds, sem, srcs, out, alu_op=0):
+        sent[0] += len(_bits(mask))
+        return RemoteDMATransfer(dst_ids=[dst(c) for c in ds], dma_engine_mask=mask, remote_sem=sem, srcs=srcs,
+                                 dsts=[out for _ in ds], alu_op=alu_op)
+
+    def fused(transfers):
+        g.remote_dma_fused(transfers, local_sem=S.ls)
+
+    g.scalar.dma_start(T.wd[:], T.w[:]).then_inc(S.wl, 16)
+    g.sync.dma_start(T.xs[:], T.x[:]).then_inc(S.xl, 16)
+
+    k_mine = cores.index(core) % B
+    g.wait_ge(S.wl, 16)
+    fused([tr(m, ds, S["wa%d" % k_mine], [T.wd[:]], T.wland[k_mine]) for m, ds in _w_plan(topo, mem, cores, core)])
+
+    def far(k):
+        o = cores[j * B + k]
+        co, cm = topo.chip(o), topo.chip(core)
+        return 0 if o == core else 1 if co == cm else 2 if (topo.same_plane(co, cm) or topo.mates(co, cm)) else 3
+    w_order = sorted(range(B), key=far)
+    for k in w_order:
+        o = cores[j * B + k]
+        if o == core:
+            g.scalar.dma_start(blk(T.wsb, k), T.w[:]).then_inc(S["ws%d" % k], 16)
+        else:
+            cnt = sum(len(_bits(m)) for m, ds in _w_plan(topo, mem, cores, o) if core in ds)
+            g.scalar.wait_ge(S["wa%d" % k], cnt)
+            g.scalar.dma_start(blk(T.wsb, k), T.wland[k]).then_inc(S["ws%d" % k], 16)
+
+    g.wait_ge(S.xl, 16)
+    for call in _rs_plan(topo, mem, core):
+        fused([tr(m, [c], S.ra, [sl(T.xs, mem[a].index(c))], sl(T.rl, j)) for m, c in call])
+    peers = [p for p in range(G) if p != j]
+    ra_all = sum(len(_bits(m)) for p in peers for call in _rs_plan(topo, mem, mem[a][p]) for m, c in call if c == core)
+
+    others = [q for q in range(NC) if q != a]
+    far_cores = [mem[q][j] for q in others]
+    g.wait_ge(S.ra, ra_all)
+    fused([tr(_common(topo, core, far_cores), far_cores, S["xc%d" % a],
+              [sl(T.xs, j)] + [sl(T.rl, p) for p in peers], sl(T.xr, a), alu_op=1)])
+
+    te = g.tensor
+    ps = [T["ps%d" % k][:, 0:F] for k in range(B)]
+    te.wait_ge(S.xl, 16)
+    for k in w_order:
+        te.wait_ge(S["ws%d" % k], 16)
+        te.matmul(ps[k], blk(T.wsb, k), blk(T.xs, j * B + k), start=True, stop=False)
+    te.wait_ge(S.ra, ra_all)
+    for p in peers:
+        for k in range(B):
+            te.matmul(ps[k], blk(T.wsb, k), blk(T.rl, p * B + k), start=False, stop=False)
+    others.sort(key=lambda q: 0 if topo.same_plane(CHIPS[q], CHIPS[a]) or topo.mates(CHIPS[q], CHIPS[a]) else 1)
+    for q in others:
+        src = mem[q][j]
+        te.wait_ge(S["xc%d" % q], len(_bits(_common(topo, src, [mem[z][j] for z in range(NC) if z != q]))))
+        for k in range(B):
+            last = q == others[-1]
+            mm = te.matmul(ps[k], blk(T.wsb, k), blk(T.xr, q * B + k), start=False, stop=last)
+            if last:
+                mm.then_inc(S["mm%d" % k], 1)
+
+    for k in range(B):
+        g.vector.wait_ge(S["mm%d" % k], 1)
+        g.vector.tensor_copy(blk(T.yb, j * B + k), ps[k]).then_inc(S.cp, 1)
+
+    ring = [(j + d) % G for d in range(1, G)]
+    near = [mem[a][p] for p in ring]
+    g.wait_ge(S.cp, B)
+    fused([tr(_common(topo, core, near), near, S["ag%d" % j], [sl(T.yb, j)], sl(T.yb, j))])
+
+    g.sync.wait_ge(S.cp, B)
+    g.sync.dma_start(sl(T.y, j), sl(T.yb, j)).then_inc(S.st, 16)
+    queues = [g.scalar, g.sync, g.scalar]
+    for i, d in enumerate(range(1, G)):
+        p = (j - d) % G
+        src = mem[a][p]
+        cnt = len(_bits(_common(topo, src, [c for c in mem[a] if c != src])))
+        queues[i % len(queues)].wait_ge(S["ag%d" % p], cnt)
+        queues[i % len(queues)].dma_start(sl(T.y, p), sl(T.yb, p)).then_inc(S.st, 16)
+
+    g.wait_ge(S.ls, sent[0])
+    g.wait_ge(S.st, 16 * G)

@@ -13,27 +13,20 @@ SCRATCH = {
     "xs": ("sbuf", [128, N * F], "bfloat16"),
     "rl": ("sbuf", [128, G * W], "bfloat16"),
     "xr": ("sbuf", [128, NC * W], "bfloat16"),
-    "wd": ("dram", [128, F], "bfloat16"),
-    "wland": ("dram", [B, 128, F], "bfloat16"),
+    "wm": ("sbuf", [128, F], "bfloat16"),
     "wsb": ("sbuf", [128, W], "bfloat16"),
     "yb": ("sbuf", [128, N * F], "bfloat16"),
 }
 for _k in range(B):
     SCRATCH["ps%d" % _k] = ("psum", [128, 512], "float32")
 
-SEMAPHORES = (["xl", "wl", "ra", "cp", "st", "ls"]
-              + ["wa%d" % k for k in range(B)] + ["ws%d" % k for k in range(B)] + ["mm%d" % k for k in range(B)]
+SEMAPHORES = (["xl", "xo", "wl", "ra", "cp", "go", "st", "ls"]
+              + ["wa%d" % k for k in range(B)] + ["mm%d" % k for k in range(B)]
               + ["xc%d" % a for a in range(NC)] + ["ag%d" % p for p in range(G)])
 
 
 def _bits(mask):
     return [1 << b for b in range(mask.bit_length()) if (mask >> b) & 1]
-
-
-def _part(mask, i, n):
-    bits = _bits(mask)
-    m = len(bits) // n
-    return sum(bits[i * m:(i + 1) * m])
 
 
 def _common(topo, src, dsts):
@@ -60,14 +53,12 @@ def _w_plan(topo, mem, cores, src):
 
 def _rs_plan(topo, mem, src):
     peers = [c for c in mem[CHIPS.index(topo.chip(src))] if c != src]
-    calls = []
-    for grp in ([c for c in peers if topo.die(c) != topo.die(src)], [c for c in peers if topo.die(c) == topo.die(src)]):
-        if grp:
-            n = 1
-            while n < len(grp):
-                n *= 2
-            calls.append([(_part(topo.mask(src, c), i, n), c) for i, c in enumerate(grp)])
-    return calls
+    bits = _bits(_common(topo, src, peers))
+    far = [c for c in peers if topo.die(c) != topo.die(src)]
+    near = [c for c in peers if topo.die(c) == topo.die(src)]
+    ev, od = bits[0::2], bits[1::2]
+    m = len(ev) // len(far)
+    return [(sum(ev[i * m:(i + 1) * m]), c) for i, c in enumerate(far)] + [(sum(od), near[0])]
 
 
 def rank_program(g, core, T, topo):
@@ -99,56 +90,56 @@ def rank_program(g, core, T, topo):
     def fused(transfers):
         g.remote_dma_fused(transfers, local_sem=S.ls)
 
-    g.scalar.dma_start(T.wd[:], T.w[:]).then_inc(S.wl, 16)
-    g.sync.dma_start(T.xs[:], T.x[:]).then_inc(S.xl, 16)
+    g.scalar.dma_start(T.wm[:], T.w[:]).then_inc(S.wl, 16)
+    pieces = sorted([(lo, hi) for lo, hi in ((0, j * W), ((j + 1) * W, G * W)) if hi > lo], key=lambda p: p[0] - p[1])
+    for q, (lo, hi) in zip([g.sync, g.scalar], pieces):
+        q.dma_start(T.xs[:, lo:hi], T.x[:, lo:hi]).then_inc(S.xl, 16)
+    g.sync.dma_start(sl(T.xs, j), sl(T.x, j)).then_inc(S.xo, 16)
 
     k_mine = cores.index(core) % B
     g.wait_ge(S.wl, 16)
-    fused([tr(m, ds, S["wa%d" % k_mine], [T.wd[:]], T.wland[k_mine]) for m, ds in _w_plan(topo, mem, cores, core)])
+    fused([tr(m, ds, S["wa%d" % k_mine], [T.wm[:]], blk(T.wsb, k_mine)) for m, ds in _w_plan(topo, mem, cores, core)])
+
+    g.wait_ge(S.xl, 16 * len(pieces))
+    fused([tr(m, [c], S.ra, [sl(T.xs, mem[a].index(c))], sl(T.rl, j)) for m, c in _rs_plan(topo, mem, core)])
+    peers = [p for p in range(G) if p != j]
+    ra_all = sum(len(_bits(m)) for p in peers for m, c in _rs_plan(topo, mem, mem[a][p]) if c == core)
+
+    def ring_of(q):
+        return [(q + d) % NC for d in range(1, NC)]
+    far_cores = [mem[q][j] for q in ring_of(a)]
+    g.wait_ge(S.xo, 16)
+    g.wait_ge(S.ra, ra_all)
+    fused([tr(_common(topo, core, far_cores), far_cores, S["xc%d" % a],
+              [sl(T.xs, j)] + [sl(T.rl, p) for p in peers], sl(T.xr, a), alu_op=1)])
 
     def far(k):
         o = cores[j * B + k]
         co, cm = topo.chip(o), topo.chip(core)
         return 0 if o == core else 1 if co == cm else 2 if (topo.same_plane(co, cm) or topo.mates(co, cm)) else 3
-    w_order = sorted(range(B), key=far)
-    for k in w_order:
-        o = cores[j * B + k]
-        if o == core:
-            g.scalar.dma_start(blk(T.wsb, k), T.w[:]).then_inc(S["ws%d" % k], 16)
-        else:
-            cnt = sum(len(_bits(m)) for m, ds in _w_plan(topo, mem, cores, o) if core in ds)
-            g.scalar.wait_ge(S["wa%d" % k], cnt)
-            g.scalar.dma_start(blk(T.wsb, k), T.wland[k]).then_inc(S["ws%d" % k], 16)
 
-    g.wait_ge(S.xl, 16)
-    for call in _rs_plan(topo, mem, core):
-        fused([tr(m, [c], S.ra, [sl(T.xs, mem[a].index(c))], sl(T.rl, j)) for m, c in call])
-    peers = [p for p in range(G) if p != j]
-    ra_all = sum(len(_bits(m)) for p in peers for call in _rs_plan(topo, mem, mem[a][p]) for m, c in call if c == core)
-
-    others = [q for q in range(NC) if q != a]
-    far_cores = [mem[q][j] for q in others]
-    g.wait_ge(S.ra, ra_all)
-    fused([tr(_common(topo, core, far_cores), far_cores, S["xc%d" % a],
-              [sl(T.xs, j)] + [sl(T.rl, p) for p in peers], sl(T.xr, a), alu_op=1)])
+    def wk(k):
+        return T.wm[:] if cores[j * B + k] == core else blk(T.wsb, k)
 
     te = g.tensor
     ps = [T["ps%d" % k][:, 0:F] for k in range(B)]
-    te.wait_ge(S.xl, 16)
-    for k in w_order:
-        te.wait_ge(S["ws%d" % k], 16)
-        te.matmul(ps[k], blk(T.wsb, k), blk(T.xs, j * B + k), start=True, stop=False)
+    te.wait_ge(S.xo, 16)
     te.wait_ge(S.ra, ra_all)
-    for p in peers:
+    for k in sorted(range(B), key=far):
+        o = cores[j * B + k]
+        if o == core:
+            te.wait_ge(S.wl, 16)
+        else:
+            te.wait_ge(S["wa%d" % k], sum(len(_bits(m)) for m, ds in _w_plan(topo, mem, cores, o) if core in ds))
+        te.matmul(ps[k], wk(k), blk(T.xs, j * B + k), start=True, stop=False)
+        for p in peers:
+            te.matmul(ps[k], wk(k), blk(T.rl, p * B + k), start=False, stop=False)
+    comers = sorted(ring_of(a), key=lambda q: ring_of(q).index(a))
+    for q in comers:
+        te.wait_ge(S["xc%d" % q], len(_bits(_common(topo, mem[q][j], [mem[z][j] for z in ring_of(q)]))))
         for k in range(B):
-            te.matmul(ps[k], blk(T.wsb, k), blk(T.rl, p * B + k), start=False, stop=False)
-    others.sort(key=lambda q: 0 if topo.same_plane(CHIPS[q], CHIPS[a]) or topo.mates(CHIPS[q], CHIPS[a]) else 1)
-    for q in others:
-        src = mem[q][j]
-        te.wait_ge(S["xc%d" % q], len(_bits(_common(topo, src, [mem[z][j] for z in range(NC) if z != q]))))
-        for k in range(B):
-            last = q == others[-1]
-            mm = te.matmul(ps[k], blk(T.wsb, k), blk(T.xr, q * B + k), start=False, stop=last)
+            last = q == comers[-1]
+            mm = te.matmul(ps[k], wk(k), blk(T.xr, q * B + k), start=False, stop=last)
             if last:
                 mm.then_inc(S["mm%d" % k], 1)
 
@@ -160,8 +151,10 @@ def rank_program(g, core, T, topo):
     near = [mem[a][p] for p in ring]
     g.wait_ge(S.cp, B)
     fused([tr(_common(topo, core, near), near, S["ag%d" % j], [sl(T.yb, j)], sl(T.yb, j))])
+    g.sem_inc(S.go, 1)
 
     g.sync.wait_ge(S.cp, B)
+    g.sync.wait_ge(S.go, 1)
     g.sync.dma_start(sl(T.y, j), sl(T.yb, j)).then_inc(S.st, 16)
     queues = [g.scalar, g.sync, g.scalar]
     for i, d in enumerate(range(1, G)):

@@ -20,7 +20,7 @@ SCRATCH = {
 for _k in range(B):
     SCRATCH["ps%d" % _k] = ("psum", [128, 512], "float32")
 
-SEMAPHORES = (["xl", "xo", "wl", "ra", "cp", "go", "st", "ls"]
+SEMAPHORES = (["x0", "x1", "x2", "xo", "wl", "ra", "cp", "go", "st", "ls"]
               + ["wa%d" % k for k in range(B)] + ["mm%d" % k for k in range(B)]
               + ["xc%d" % a for a in range(NC)] + ["ag%d" % p for p in range(G)])
 
@@ -40,25 +40,30 @@ def _members(topo, cores):
     return [sorted([c for c in cores if topo.chip(c) == ch], key=lambda c: (topo.die(c), c)) for ch in CHIPS]
 
 
+def _engines(topo, cores, src):
+    on = _bits(_common(topo, src, [c for c in cores if c != src and topo.chip(c) == topo.chip(src)]))
+    out = _common(topo, src, [c for c in cores if topo.chip(c) != topo.chip(src)])
+    rest = on[1::2]
+    return {"far": sum(on[0::2]), "woff": sum(b for b in rest if b & out), "near": sum(b for b in rest if not b & out),
+            "late": sum(b for b in on if not b & out)}
+
+
 def _w_plan(topo, mem, cores, src):
     jr = cores.index(src) // B
     dests = [mem[a][jr] for a in range(NC) if mem[a][jr] != src]
-    off = [d for d in dests if topo.chip(d) != topo.chip(src)]
-    on = [d for d in dests if topo.chip(d) == topo.chip(src)]
-    plan = [(_common(topo, src, off), off)]
-    if on:
-        plan.append((_common(topo, src, on) & ~plan[0][0], on))
-    return plan
+    e = _engines(topo, cores, src)
+    return ((e["woff"], [d for d in dests if topo.chip(d) != topo.chip(src)]),
+            (e["late"], [d for d in dests if topo.chip(d) == topo.chip(src)]))
 
 
-def _rs_plan(topo, mem, src):
-    peers = [c for c in mem[CHIPS.index(topo.chip(src))] if c != src]
-    bits = _bits(_common(topo, src, peers))
-    far = [c for c in peers if topo.die(c) != topo.die(src)]
-    near = [c for c in peers if topo.die(c) == topo.die(src)]
-    ev, od = bits[0::2], bits[1::2]
-    m = len(ev) // len(far)
-    return [(sum(ev[i * m:(i + 1) * m]), c) for i, c in enumerate(far)] + [(sum(od), near[0])]
+def _rs_plan(topo, mem, cores, src):
+    mine = mem[CHIPS.index(topo.chip(src))]
+    far = [c for c in mine if topo.die(c) != topo.die(src)]
+    same = [c for c in mine if topo.die(c) == topo.die(src)]
+    if same.index(src) % 2:
+        far = far[::-1]
+    e = _engines(topo, cores, src)
+    return [(e["far"], far[0]), (e["near"], [c for c in same if c != src][0]), (e["far"], far[1])]
 
 
 def rank_program(g, core, T, topo):
@@ -90,20 +95,25 @@ def rank_program(g, core, T, topo):
     def fused(transfers):
         g.remote_dma_fused(transfers, local_sem=S.ls)
 
-    g.scalar.dma_start(T.wm[:], T.w[:]).then_inc(S.wl, 16)
-    pieces = sorted([(lo, hi) for lo, hi in ((0, j * W), ((j + 1) * W, G * W)) if hi > lo], key=lambda p: p[0] - p[1])
-    for q, (lo, hi) in zip([g.sync, g.scalar], pieces):
-        q.dma_start(T.xs[:, lo:hi], T.x[:, lo:hi]).then_inc(S.xl, 16)
+    plan = _rs_plan(topo, mem, cores, core)
+    g.sync.dma_start(T.wm[:], T.w[:]).then_inc(S.wl, 16)
+    for i, (m, c) in enumerate(plan):
+        p = mem[a].index(c)
+        g.sync.dma_start(sl(T.xs, p), sl(T.x, p)).then_inc(S["x%d" % i], 16)
     g.sync.dma_start(sl(T.xs, j), sl(T.x, j)).then_inc(S.xo, 16)
 
     k_mine = cores.index(core) % B
+    (w_off_m, w_off), (w_on_m, w_on) = _w_plan(topo, mem, cores, core)
     g.wait_ge(S.wl, 16)
-    fused([tr(m, ds, S["wa%d" % k_mine], [T.wm[:]], blk(T.wsb, k_mine)) for m, ds in _w_plan(topo, mem, cores, core)])
+    fused([tr(w_off_m, w_off, S["wa%d" % k_mine], [T.wm[:]], blk(T.wsb, k_mine))])
 
-    g.wait_ge(S.xl, 16 * len(pieces))
-    fused([tr(m, [c], S.ra, [sl(T.xs, mem[a].index(c))], sl(T.rl, j)) for m, c in _rs_plan(topo, mem, core)])
+    for i, (m, c) in enumerate(plan):
+        g.wait_ge(S["x%d" % i], 16)
+        fused([tr(m, [c], S.ra, [sl(T.xs, mem[a].index(c))], sl(T.rl, j))])
+    if w_on:
+        fused([tr(w_on_m, w_on, S["wa%d" % k_mine], [T.wm[:]], blk(T.wsb, k_mine))])
     peers = [p for p in range(G) if p != j]
-    ra_all = sum(len(_bits(m)) for p in peers for m, c in _rs_plan(topo, mem, mem[a][p]) if c == core)
+    ra_all = sum(len(_bits(m)) for p in peers for m, c in _rs_plan(topo, mem, cores, mem[a][p]) if c == core)
 
     def ring_of(q):
         return [(q + d) % NC for d in range(1, NC)]
@@ -153,16 +163,18 @@ def rank_program(g, core, T, topo):
     fused([tr(_common(topo, core, near), near, S["ag%d" % j], [sl(T.yb, j)], sl(T.yb, j))])
     g.sem_inc(S.go, 1)
 
+    def landed(q, p):
+        src = mem[a][p]
+        q.wait_ge(S["ag%d" % p], len(_bits(_common(topo, src, [c for c in mem[a] if c != src]))))
+
+    order = [(j - d) % G for d in range(1, G)]
     g.sync.wait_ge(S.cp, B)
     g.sync.wait_ge(S.go, 1)
+    landed(g.sync, order[0])
     g.sync.dma_start(sl(T.y, j), sl(T.yb, j)).then_inc(S.st, 16)
-    queues = [g.scalar, g.sync, g.scalar]
-    for i, d in enumerate(range(1, G)):
-        p = (j - d) % G
-        src = mem[a][p]
-        cnt = len(_bits(_common(topo, src, [c for c in mem[a] if c != src])))
-        queues[i % len(queues)].wait_ge(S["ag%d" % p], cnt)
-        queues[i % len(queues)].dma_start(sl(T.y, p), sl(T.yb, p)).then_inc(S.st, 16)
+    for q, p in zip([g.scalar, g.sync, g.scalar], order):
+        landed(q, p)
+        q.dma_start(sl(T.y, p), sl(T.yb, p)).then_inc(S.st, 16)
 
     g.wait_ge(S.ls, sent[0])
     g.wait_ge(S.st, 16 * G)

import comms_topo
from concourse.bass import DstId, RemoteDMATransfer

N, F = 12, 128
CORES = [2, 3, 6, 7, 58, 59, 62, 63, 114, 115, 118, 119]
CHIPS = sorted({comms_topo.chip(c) for c in CORES})
NC = len(CHIPS)
G = N // NC
B = N // G
W = B * F

SCRATCH = {
    "xs": ("sbuf", [128, N * F], "bfloat16"),
    "rl": ("sbuf", [128, G * W], "bfloat16"),
    "xr": ("sbuf", [128, NC * W], "bfloat16"),
    "wm": ("sbuf", [128, F], "bfloat16"),
    "wsb": ("sbuf", [128, W], "bfloat16"),
    "yb": ("sbuf", [128, N * F], "bfloat16"),
}
for _k in range(B):
    SCRATCH["ps%d" % _k] = ("psum", [128, 512], "float32")

SEMAPHORES = (["x0", "x1", "x2", "xo", "wl", "ra", "cp", "go", "st", "ls"]
              + ["wa%d" % k for k in range(B)] + ["mm%d" % k for k in range(B)]
              + ["xc%d" % a for a in range(NC)] + ["ag%d" % p for p in range(G)])


def _bits(mask):
    return [1 << b for b in range(mask.bit_length()) if (mask >> b) & 1]


def _common(topo, src, dsts):
    m = topo.mask(src, dsts[0])
    for d in dsts[1:]:
        m &= topo.mask(src, d)
    return m


def _members(topo, cores):
    return [sorted([c for c in cores if topo.chip(c) == ch], key=lambda c: (topo.die(c), c)) for ch in CHIPS]


def _engines(topo, cores, src):
    on = _bits(_common(topo, src, [c for c in cores if c != src and topo.chip(c) == topo.chip(src)]))
    out = _common(topo, src, [c for c in cores if topo.chip(c) != topo.chip(src)])
    rest = on[1::2]
    return {"far": sum(on[0::2]), "woff": sum(b for b in rest if b & out), "near": sum(b for b in rest if not b & out),
            "late": sum(b for b in on if not b & out)}


def _w_plan(topo, mem, cores, src):
    jr = cores.index(src) // B
    dests = [mem[a][jr] for a in range(NC) if mem[a][jr] != src]
    e = _engines(topo, cores, src)
    return ((e["woff"], [d for d in dests if topo.chip(d) != topo.chip(src)]),
            (e["late"], [d for d in dests if topo.chip(d) == topo.chip(src)]))


def _rs_plan(topo, mem, cores, src):
    mine = mem[CHIPS.index(topo.chip(src))]
    far = [c for c in mine if topo.die(c) != topo.die(src)]
    same = [c for c in mine if topo.die(c) == topo.die(src)]
    if same.index(src) % 2:
        far = far[::-1]
    e = _engines(topo, cores, src)
    return [(e["far"], far[0]), (e["near"], [c for c in same if c != src][0]), (e["far"], far[1])]


def rank_program(g, core, T, topo):
    if T.rank_of(core) is None:
        return
    cores = list(T.cores)
    mem = _members(topo, cores)
    a = CHIPS.index(topo.chip(core))
    j = mem[a].index(core)
    S = T.sem
    sent = [0]

    def dst(c):
        assert topo.may_write(core, c)
        rid, pid, _ = topo.addr(c)
        return DstId(rid=rid, pnc=pid)

    def sl(t, i):
        return t[:, i * W:(i + 1) * W]

    def blk(t, i):
        return t[:, i * F:(i + 1) * F]

    def tr(mask, ds, sem, srcs, out, alu_op=0):
        sent[0] += len(_bits(mask))
        return RemoteDMATransfer(dst_ids=[dst(c) for c in ds], dma_engine_mask=mask, remote_sem=sem, srcs=srcs,
                                 dsts=[out for _ in ds], alu_op=alu_op)

    def fused(transfers):
        g.remote_dma_fused(transfers, local_sem=S.ls)

    plan = _rs_plan(topo, mem, cores, core)
    g.sync.dma_start(T.wm[:], T.w[:]).then_inc(S.wl, 16)
    for i, (m, c) in enumerate(plan):
        p = mem[a].index(c)
        g.sync.dma_start(sl(T.xs, p), sl(T.x, p)).then_inc(S["x%d" % i], 16)
    g.sync.dma_start(sl(T.xs, j), sl(T.x, j)).then_inc(S.xo, 16)

    k_mine = cores.index(core) % B
    (w_off_m, w_off), (w_on_m, w_on) = _w_plan(topo, mem, cores, core)
    g.wait_ge(S.wl, 16)
    fused([tr(w_off_m, w_off, S["wa%d" % k_mine], [T.wm[:]], blk(T.wsb, k_mine))])

    for i, (m, c) in enumerate(plan):
        g.wait_ge(S["x%d" % i], 16)
        fused([tr(m, [c], S.ra, [sl(T.xs, mem[a].index(c))], sl(T.rl, j))])
    if w_on:
        fused([tr(w_on_m, w_on, S["wa%d" % k_mine], [T.wm[:]], blk(T.wsb, k_mine))])
    peers = [p for p in range(G) if p != j]
    ra_all = sum(len(_bits(m)) for p in peers for m, c in _rs_plan(topo, mem, cores, mem[a][p]) if c == core)

    def ring_of(q):
        return [(q + d) % NC for d in range(1, NC)]
    far_cores = [mem[q][j] for q in ring_of(a)]
    g.wait_ge(S.xo, 16)
    g.wait_ge(S.ra, ra_all)
    fused([tr(_common(topo, core, far_cores), far_cores, S["xc%d" % a],
              [sl(T.xs, j)] + [sl(T.rl, p) for p in peers], sl(T.xr, a), alu_op=1)])

    def far(k):
        o = cores[j * B + k]
        co, cm = topo.chip(o), topo.chip(core)
        return 0 if o == core else 1 if co == cm else 2 if (topo.same_plane(co, cm) or topo.mates(co, cm)) else 3

    def wk(k):
        return T.wm[:] if cores[j * B + k] == core else blk(T.wsb, k)

    te = g.tensor
    ps = [T["ps%d" % k][:, 0:F] for k in range(B)]
    te.wait_ge(S.xo, 16)
    te.wait_ge(S.ra, ra_all)
    for k in sorted(range(B), key=far):
        o = cores[j * B + k]
        if o == core:
            te.wait_ge(S.wl, 16)
        else:
            te.wait_ge(S["wa%d" % k], sum(len(_bits(m)) for m, ds in _w_plan(topo, mem, cores, o) if core in ds))
        te.matmul(ps[k], wk(k), blk(T.xs, j * B + k), start=True, stop=False)
        for p in peers:
            te.matmul(ps[k], wk(k), blk(T.rl, p * B + k), start=False, stop=False)
    comers = sorted(ring_of(a), key=lambda q: ring_of(q).index(a))
    for q in comers:
        te.wait_ge(S["xc%d" % q], len(_bits(_common(topo, mem[q][j], [mem[z][j] for z in ring_of(q)]))))
        for k in range(B):
            last = q == comers[-1]
            mm = te.matmul(ps[k], wk(k), blk(T.xr, q * B + k), start=False, stop=last)
            if last:
                mm.then_inc(S["mm%d" % k], 1)

    for k in range(B):
        g.vector.wait_ge(S["mm%d" % k], 1)
        g.vector.tensor_copy(blk(T.yb, j * B + k), ps[k]).then_inc(S.cp, 1)

    ring = [(j + d) % G for d in range(1, G)]
    near = [mem[a][p] for p in ring]
    g.wait_ge(S.cp, B)
    fused([tr(_common(topo, core, near), near, S["ag%d" % j], [sl(T.yb, j)], sl(T.yb, j))])
    g.sem_inc(S.go, 1)

    def landed(q, p):
        src = mem[a][p]
        q.wait_ge(S["ag%d" % p], len(_bits(_common(topo, src, [c for c in mem[a] if c != src]))))

    order = [(j - d) % G for d in range(1, G)]
    g.sync.wait_ge(S.cp, B)
    g.sync.wait_ge(S.go, 1)
    landed(g.sync, order[0])
    g.sync.dma_start(sl(T.y, j), sl(T.yb, j)).then_inc(S.st, 16)
    for q, p in zip([g.scalar, g.sync, g.scalar], order):
        landed(q, p)
        q.dma_start(sl(T.y, p), sl(T.yb, p)).then_inc(S.st, 16)

    g.wait_ge(S.ls, sent[0])
    g.wait_ge(S.st, 16 * G)
